import numpy as np
import ml_dtypes


def mxq(x, axis, fmt="e4m3"):
    dtype, down = {"e4m3": (ml_dtypes.float8_e4m3fn, 7), "e5m2": (ml_dtypes.float8_e5m2, 14)}[fmt]
    v = np.moveaxis(np.asarray(x, np.float32).astype(ml_dtypes.bfloat16).astype(np.float64), axis, -1)
    blocks = v.reshape(v.shape[:-1] + (-1, 32))
    amax = np.abs(blocks).max(-1, keepdims=True)
    byte = np.maximum(np.where(amax > 0, np.frexp(amax)[1] - 1 + 127, 0) - down, 1)
    scale = np.exp2(byte - 127.0)
    codes = (blocks / scale).astype(np.float32).astype(dtype).astype(np.float64)
    return np.moveaxis((codes * scale).reshape(v.shape), -1, axis)


WIDE = False


def mx_kscale(k):
    if not WIDE:
        return np.ones(k)
    levels = np.array([10, -10, 5, -5, 0])
    if k % 512:
        return np.exp2(np.random.permutation(np.resize(levels, k // 32))).repeat(32)
    a = np.empty((k // 512, 16))
    for p in range(k // 512):
        a[p, :8] = np.random.permutation(np.resize(levels, 8))
        for g in range(8):
            far = levels[np.abs(levels - a[p, g]) >= 10]
            a[p, g + 8] = far[np.random.randint(len(far))]
    return np.exp2(a.ravel()).repeat(32)


def f64(x):
    return np.asarray(x).astype(np.float64)


def striped8(idx):
    return np.asarray(idx).reshape(8, -1, 16).transpose(0, 2, 1).reshape(128, -1).astype(np.uint16)


def unstriped8(offs):
    return offs.reshape(8, 16, -1).transpose(0, 2, 1).reshape(8, -1).astype(np.int64)


def pick8(x, idx, run):
    r = np.arange(len(x))
    return x[r[:, None], idx[r % (8 * run) // run]]


E2M1 = np.array([0.0, 0.5, 1.0, 1.5, 2.0, 3.0, 4.0, 6.0, -0.0, -0.5, -1.0, -1.5, -2.0, -3.0, -4.0, -6.0])


def pack_weight(w, fmt):
    k, n = w.shape
    w = f64(np.asarray(w, np.float32).astype(ml_dtypes.bfloat16)).reshape(k // 32, 32, n)
    amax = np.abs(w).max(1)
    if fmt == "e4m3":
        byte = np.frexp(amax)[1] - 1 + 127 - 7
    else:
        mant, ex = np.frexp(amax / 6.0)
        byte = np.where(mant > 0.5, ex, ex - 1) + 127
    byte = np.clip(np.where(amax > 0, byte, 1), 1, 254)
    scaled = (w * np.exp2(127.0 - byte)[:, None, :]).reshape(k, n).astype(np.float32)
    by_word = np.ascontiguousarray(scaled.reshape(k // 512, 128, 4, n).transpose(0, 1, 3, 2))
    if fmt == "e4m3":
        words = by_word.astype(ml_dtypes.float8_e4m3fn).view(np.uint8)
    else:
        c = by_word.astype(ml_dtypes.float4_e2m1fn).view(np.uint8) & 0xF
        words = (c[..., 0::2] | (c[..., 1::2] << 4)).reshape(k // 512, 128, 2 * n)
    return np.ascontiguousarray(words), np.ascontiguousarray(byte.astype(np.uint8).reshape(k // 512, 16, n))


def unpack_weight(words, scales, fmt):
    g, _, n = scales.shape
    words = np.ascontiguousarray(words).reshape(g, 128, n, -1)
    if fmt == "e4m3":
        vals = words.view(ml_dtypes.float8_e4m3fn).astype(np.float64)
    else:
        nib = np.empty((g, 128, n, 4), np.uint8)
        nib[..., 0::2] = words & 0xF
        nib[..., 1::2] = words >> 4
        vals = E2M1[nib]
    vals = vals * np.repeat(np.exp2(scales.astype(np.float64) - 127.0), 8, axis=1)[..., None]
    return vals.transpose(0, 1, 3, 2).reshape(g * 512, n)


D, V, Q, I = 512, 2048, 128, 512


def setup_inputs():
    n = np.random.standard_normal
    idx = np.stack([np.random.permutation(V)[:I] for _ in range(8)])
    fd = mx_kscale(D)
    vocp = pack_weight(n((D, V)) / fd[:, None], "e2m1")
    return {
        "hid": (n((D, Q)) * 0.7 / np.sqrt(D) * fd[:, None]).astype(np.float32),
        "voc_words": vocp[0],
        "voc_scales": vocp[1],
        "lpo": (np.random.uniform(-8.2, -7.2, (Q, I))).astype(np.float32),
        "adv": (1.0 * n((Q, I))).astype(np.float32),
        "dhid": (n((D, Q)) * 1.0 / np.sqrt(D) * fd[:, None]).astype(np.float32),
        "base": (0.5 * n((Q, V))).astype(np.float32),
        "offs": striped8(idx),
    }


def reference(hid, voc_words, voc_scales, lpo, adv, dhid, base, offs):
    idx = unstriped8(offs)
    vocu = unpack_weight(voc_words, voc_scales, "e2m1")
    hidq = mxq(f64(hid), 0, "e4m3")
    a = hidq.T @ vocu
    dhidq = mxq(f64(dhid), 0, "e4m3")
    ta = dhidq.T @ vocu
    p = np.exp(a)
    z = np.sum(p, axis=1, keepdims=True)
    r = np.exp(pick8(a, idx, 16) - np.log(z) - f64(lpo))
    dz = np.sum(f64(adv) * r * (-1.0), axis=1, keepdims=True) / z
    xp = ta * p
    xz = np.sum(xp, axis=1, keepdims=True)
    xr = (pick8(ta, idx, 16) - xz / z) * r
    xdz = (np.sum(xr * f64(adv) * (-1.0), axis=1, keepdims=True) - xz * np.sum(f64(adv) * r * (-1.0), axis=1, keepdims=True) / z) / z
    xe1 = xr * f64(adv)
    xs1 = np.zeros((Q, V))
    xs1[np.arange(Q)[:, None], idx[np.arange(Q) % 128 // 16]] = xe1
    xda = xdz * p + xp * dz + xs1
    y = xda + f64(base)
    return y

@@ -1,0 +1,240 @@
+from contextlib import ExitStack
+
+import concourse.mybir as mybir
+from concourse.masks import make_identity
+
+D, V, Q, I = 512, 2048, 128, 512
+FLOPS = 2 * 2 * D * Q * V
+
+F32 = mybir.dt.float32
+BF16 = mybir.dt.bfloat16
+I32 = mybir.dt.int32
+U32 = mybir.dt.uint32
+U16 = mybir.dt.uint16
+U8 = mybir.dt.uint8
+FP8X4 = mybir.dt.float8_e4m3fn_x4
+FP4X4 = mybir.dt.float4_e2m1fn_x4
+ALU = mybir.AluOpType
+ACT = mybir.ActivationFunctionType
+AX = mybir.AxisListType
+
+P = 128
+PACK = 4
+BANK = 512
+CHUNKS = V // BANK
+SPLIT = 96
+
+
+def tile_attend_hvpolicyratio_heads_kernel(tc, hid, voc_words, voc_scales, lpo, adv, dhid, base, offs, out):
+    nc = tc.nc
+    with ExitStack() as ctx:
+        keep = ctx.enter_context(tc.tile_pool(name="keep", bufs=1))
+        psum = ctx.enter_context(tc.psum_pool(name="psum", bufs=1))
+
+        voc_sc = keep.tile([P, V], U8, name="voc_sc", align_bytes=64)
+        nc.gpsimd.memset(voc_sc[:].bitcast(I32), 0)
+        xs1 = keep.tile([P, V], F32, name="xs1")
+        nc.vector.memset(xs1[:], 0.0)
+        ident = keep.tile([P, P], F32, name="ident")
+        make_identity(nc, ident[:])
+
+        hid_raw = keep.tile([P, PACK, Q], F32, name="hid_raw")
+        nc.sync.dma_start(out=hid_raw[:], in_=hid.rearrange("(p j) q -> p j q", j=PACK))
+        halves = [keep.tile([P, V], U8, name="words%d" % h, align_bytes=64) for h in range(2)]
+        nc.sync.dma_start(out=halves[0][:], in_=voc_words[0, :, 0:V])
+        for quad in range(4):
+            nc.sync.dma_start(
+                out=voc_sc[32 * quad : 32 * quad + 4, :].bitcast(I32),
+                in_=voc_scales[0, 4 * quad : 4 * quad + 4, :].bitcast(I32),
+            )
+        dhid_raw = keep.tile([P, PACK, Q], F32, name="dhid_raw")
+        nc.sync.dma_start(out=dhid_raw[:], in_=dhid.rearrange("(p j) q -> p j q", j=PACK))
+        nc.sync.dma_start(out=halves[1][:], in_=voc_words[0, :, V : 2 * V])
+        words = [halves[c // 2][:, 2 * BANK * (c % 2) : 2 * BANK * (c % 2 + 1)] for c in range(CHUNKS)]
+        offsets = keep.tile([P, I // 16], U16, name="offsets")
+        nc.sync.dma_start(offsets[:], offs)
+
+        lpo_sb = keep.tile([P, I], F32, name="lpo_sb")
+        nc.sync.dma_start(out=lpo_sb[:], in_=lpo)
+        adv_sb = keep.tile([P, I], F32, name="adv_sb")
+        nc.sync.dma_start(out=adv_sb[:], in_=adv)
+        base_sb = keep.tile([P, V], F32, name="base_sb")
+        nc.sync.dma_start(out=base_sb[:], in_=base)
+
+
+        def quantise(grouped, name):
+            codes = keep.tile([P, Q], U32, name=name + "_codes", align_bytes=64)
+            scales = keep.tile([P, Q], U8, name=name + "_scales", align_bytes=64)
+            nc.vector.quantize_mx(
+                out=codes[:].bitcast(FP8X4), scales=scales[:], in_=grouped[:].rearrange("p q j -> p (q j)")
+            )
+            return codes, scales
+
+        hid_bf = keep.tile([P, Q, PACK], BF16, name="hid_bf", align_bytes=64)
+        nc.vector.tensor_copy(out=hid_bf[:, :SPLIT, :], in_=hid_raw[:, :, :SPLIT].rearrange("p j q -> p q j"))
+        nc.scalar.activation(
+            out=hid_bf[:, SPLIT:, :], in_=hid_raw[:, :, SPLIT:].rearrange("p j q -> p q j"), func=ACT.Copy
+        )
+        hid_q = quantise(hid_bf, "hid")
+        dhid_bf = keep.tile([P, Q, PACK], BF16, name="dhid_bf", align_bytes=64)
+        nc.scalar.activation(out=dhid_bf[:], in_=dhid_raw[:].rearrange("p j q -> p q j"), func=ACT.Copy)
+        dhid_q = quantise(dhid_bf, "dhid")
+
+        def cols(c):
+            return slice(c * BANK, (c + 1) * BANK)
+
+        def score(q_operand, c, name):
+            bank = psum.tile([P, BANK], F32, name=name, tag=name)
+            nc.tensor.matmul_mx(
+                out=bank[:],
+                lhsT=q_operand[0][:].bitcast(FP8X4),
+                lhsT_scale=q_operand[1][:],
+                rhs=words[c].bitcast(FP4X4),
+                rhs_scale=voc_sc[:, cols(c)],
+                start=True,
+                stop=True,
+            )
+            return bank
+
+        a_ps = [score(hid_q, c, "a_ps%d" % c) for c in range(CHUNKS)]
+        ta_ps = {c: score(dhid_q, c, "ta_ps%d" % c) for c in (2, 0, 3, 1)}
+
+        def column(name, width=1):
+            return keep.tile([P, width], F32, name=name)
+
+        a_sb = keep.tile([P, V], F32, name="a_sb")
+        p_sb = keep.tile([P, V], F32, name="p_sb")
+        chunk_max = column("chunk_max", CHUNKS)
+        z_part = column("z_part", CHUNKS)
+        for c in range(CHUNKS):
+            nc.vector.tensor_scalar(
+                out=a_sb[:, cols(c)], in0=a_ps[c][:], scalar1=1.0, scalar2=None,
+                op0=ALU.mult, op1=ALU.max, accum_out=chunk_max[:, c : c + 1],
+            )
+            neg_chunk_max = keep.tile([P, 1], F32, name="neg_chunk_max%d" % c, tag="bias%d" % c)
+            nc.gpsimd.tensor_scalar(
+                out=neg_chunk_max[:], in0=chunk_max[:, c : c + 1], scalar1=-1.0, scalar2=0.0,
+                op0=ALU.mult, op1=ALU.add,
+            )
+            nc.scalar.activation(
+                out=p_sb[:, cols(c)], in_=a_sb[:, cols(c)], func=ACT.Exp, bias=neg_chunk_max[:],
+                accum_out=z_part[:, c : c + 1],
+            )
+        neg_max = column("neg_max")
+        nc.vector.tensor_reduce(out=neg_max[:], in_=chunk_max[:], axis=AX.X, op=ALU.max, negate=True)
+
+        x_sb = keep.tile([P, I], F32, name="x_sb")
+        nc.vector.tensor_tensor(x_sb[:], a_sb[:].indirect(offsets[:]), lpo_sb[:], ALU.subtract)
+
+        lift = column("lift", CHUNKS)
+        nc.scalar.activation(out=lift[:], in_=chunk_max[:], func=ACT.Exp, bias=neg_max[:])
+        z_lifted = column("z_lifted", CHUNKS)
+        z = column("z")
+        nc.vector.scalar_tensor_tensor(
+            out=z_lifted[:], in0=z_part[:], scalar=1.0, in1=lift[:], op0=ALU.mult, op1=ALU.mult, accum_out=z[:]
+        )
+
+        ta_sb = keep.tile([P, V], F32, name="ta_sb", tag="bias3")
+        xp_sb = keep.tile([P, V], F32, name="xp_sb")
+        xz_part = column("xz_part", CHUNKS)
+        w_sb = keep.tile([P, I], F32, name="w_sb")
+        s1 = column("s1")
+
+        def copy_ta(c):
+            nc.scalar.copy(out=ta_sb[:, cols(c)], in_=ta_ps[c][:])
+
+        def weigh_ta(c):
+            nc.vector.scalar_tensor_tensor(
+                out=xp_sb[:, cols(c)], in0=ta_ps[c][:], scalar=1.0, in1=p_sb[:, cols(c)],
+                op0=ALU.mult, op1=ALU.mult, accum_out=xz_part[:, c : c + 1],
+            )
+
+        r_sb = keep.tile([P, I], F32, name="r_sb")
+        nc.scalar.activation(out=r_sb[:], in_=x_sb[:], func=ACT.Exp, bias=neg_max[:])
+        copy_ta(2)
+        copy_ta(3)
+        weigh_ta(0)
+        rz = column("rz")
+        nc.vector.reciprocal(out=rz[:], in_=z[:])
+        neg_share = column("neg_share", CHUNKS)
+        nc.gpsimd.tensor_scalar(
+            out=neg_share[:], in0=lift[:], scalar1=rz[:], scalar2=-1.0, op0=ALU.mult, op1=ALU.mult
+        )
+        weigh_ta(1)
+        copy_ta(0)
+        copy_ta(1)
+        nc.vector.scalar_tensor_tensor(
+            out=w_sb[:], in0=r_sb[:], scalar=rz[:], in1=adv_sb[:], op0=ALU.mult, op1=ALU.mult, accum_out=s1[:]
+        )
+        weigh_ta(2)
+        weigh_ta(3)
+
+        m_part = column("m_part", CHUNKS)
+        neg_m = column("neg_m")
+        nc.vector.scalar_tensor_tensor(
+            out=m_part[:], in0=xz_part[:], scalar=1.0, in1=neg_share[:], op0=ALU.mult, op1=ALU.mult,
+            accum_out=neg_m[:],
+        )
+        g_sb = keep.tile([P, I], F32, name="g_sb")
+        nc.vector.tensor_tensor(g_sb[:], ta_sb[:].indirect(offsets[:]), w_sb[:], ALU.mult)
+        xe1 = keep.tile([P, I], F32, name="xe1")
+        s2 = column("s2")
+        nc.vector.scalar_tensor_tensor(
+            out=xe1[:], in0=w_sb[:], scalar=neg_m[:], in1=g_sb[:], op0=ALU.mult, op1=ALU.add, accum_out=s2[:]
+        )
+        nc.vector.tensor_copy(xs1[:].indirect(offsets[:]), xe1[:])
+
+        turned = [psum.tile([P, BANK], F32, name="turned%d" % c, tag="a_ps%d" % c) for c in range(CHUNKS)]
+
+        def turn_in(c, src, start, stop):
+            for j in range(BANK // P):
+                nc.tensor.matmul(
+                    turned[c][:, j * P : (j + 1) * P], lhsT=src[:, j * P : (j + 1) * P], rhs=ident[:],
+                    is_transpose=True, start=(start and j == 0), stop=(stop and j == BANK // P - 1),
+                )
+
+        for c in range(CHUNKS):
+            turn_in(c, base_sb[:, cols(c)], True, False)
+
+        dz = column("dz", CHUNKS)
+        nc.scalar.activation(out=dz[:], in_=neg_share[:], func=ACT.Copy, scale=s1[:])
+        t1 = keep.tile([P, V], F32, name="t1")
+        for c in range(CHUNKS):
+            nc.scalar.activation(out=t1[:, cols(c)], in_=xp_sb[:, cols(c)], func=ACT.Copy, scale=dz[:, c : c + 1])
+            turn_in(c, t1[:, cols(c)], False, False)
+
+        k = column("k")
+        nc.scalar.activation(out=k[:], in_=s1[:], func=ACT.Identity, scale=neg_m[:], bias=s2[:])
+
+        xdz = column("xdz", CHUNKS)
+        nc.scalar.activation(out=xdz[:], in_=neg_share[:], func=ACT.Copy, scale=k[:])
+        t2 = keep.tile([P, V], F32, name="t2")
+        flat = keep.tile([P, V], F32, name="flat")
+
+        def scale_p(c):
+            if c < 2:
+                nc.scalar.activation(
+                    out=t2[:, cols(c)], in_=p_sb[:, cols(c)], func=ACT.Copy, scale=xdz[:, c : c + 1]
+                )
+            else:
+                nc.gpsimd.tensor_scalar(
+                    out=t2[:, cols(c)], in0=p_sb[:, cols(c)], scalar1=k[:], scalar2=neg_share[:, c : c + 1],
+                    op0=ALU.mult, op1=ALU.mult,
+                )
+            turn_in(c, t2[:, cols(c)], False, True)
+
+        def finish(c):
+            nc.scalar.copy(out=flat[:, cols(c)], in_=turned[c][:])
+            back = psum.tile([P, BANK], F32, name="back%d" % c, tag="ta_ps%d" % c)
+            for j in range(BANK // P):
+                lo = c * BANK + j * P
+                nc.tensor.transpose(back[:, j * P : (j + 1) * P], flat[:, lo : lo + P], ident[:])
+            res = keep.tile([P, BANK], F32, name="res%d" % c)
+            nc.vector.tensor_tensor(res[:], back[:], xs1[:, cols(c)], ALU.add)
+            nc.sync.dma_start(out=out[:, cols(c)], in_=res[:])
+
+        scale_p(0)
+        for c in range(CHUNKS):
+            if c + 1 < CHUNKS:
+                scale_p(c + 1)
+            finish(c)

@@ -22,7 +22,8 @@ P = 128
 PACK = 4
 BANK = 512
 CHUNKS = V // BANK
-SPLIT = 96
+SPLIT = 112
+DIRECT = 1
 
 
 def tile_attend_hvpolicyratio_heads_kernel(tc, hid, voc_words, voc_scales, lpo, adv, dhid, base, offs, out):
@@ -32,7 +33,7 @@ def tile_attend_hvpolicyratio_heads_kernel(tc, hid, voc_words, voc_scales, lpo, 
         psum = ctx.enter_context(tc.psum_pool(name="psum", bufs=1))
 
         voc_sc = keep.tile([P, V], U8, name="voc_sc", align_bytes=64)
-        nc.gpsimd.memset(voc_sc[:].bitcast(I32), 0)
+        nc.vector.memset(voc_sc[:].bitcast(I32), 0)
         xs1 = keep.tile([P, V], F32, name="xs1")
         nc.vector.memset(xs1[:], 0.0)
         ident = keep.tile([P, P], F32, name="ident")
@@ -76,7 +77,7 @@ def tile_attend_hvpolicyratio_heads_kernel(tc, hid, voc_words, voc_scales, lpo, 
             out=hid_bf[:, SPLIT:, :], in_=hid_raw[:, :, SPLIT:].rearrange("p j q -> p q j"), func=ACT.Copy
         )
         hid_q = quantise(hid_bf, "hid")
-        dhid_bf = keep.tile([P, Q, PACK], BF16, name="dhid_bf", align_bytes=64)
+        dhid_bf = keep.tile([P, Q, PACK], BF16, name="dhid_bf", tag="max1", align_bytes=64)
         nc.scalar.activation(out=dhid_bf[:], in_=dhid_raw[:].rearrange("p j q -> p q j"), func=ACT.Copy)
         dhid_q = quantise(dhid_bf, "dhid")
 
@@ -104,37 +105,37 @@ def tile_attend_hvpolicyratio_heads_kernel(tc, hid, voc_words, voc_scales, lpo, 
 
         a_sb = keep.tile([P, V], F32, name="a_sb")
         p_sb = keep.tile([P, V], F32, name="p_sb")
-        chunk_max = column("chunk_max", CHUNKS)
+        neg_chunk_max = column("neg_chunk_max", CHUNKS)
         z_part = column("z_part", CHUNKS)
         for c in range(CHUNKS):
+            chunk_max = keep.tile([P, 1], F32, name="chunk_max%d" % c, tag="max%d" % c, align_bytes=64)
             nc.vector.tensor_scalar(
                 out=a_sb[:, cols(c)], in0=a_ps[c][:], scalar1=1.0, scalar2=None,
-                op0=ALU.mult, op1=ALU.max, accum_out=chunk_max[:, c : c + 1],
+                op0=ALU.mult, op1=ALU.max, accum_out=chunk_max[:],
             )
-            neg_chunk_max = keep.tile([P, 1], F32, name="neg_chunk_max%d" % c, tag="bias%d" % c)
             nc.gpsimd.tensor_scalar(
-                out=neg_chunk_max[:], in0=chunk_max[:, c : c + 1], scalar1=-1.0, scalar2=0.0,
+                out=neg_chunk_max[:, c : c + 1], in0=chunk_max[:], scalar1=-1.0, scalar2=0.0,
                 op0=ALU.mult, op1=ALU.add,
             )
             nc.scalar.activation(
-                out=p_sb[:, cols(c)], in_=a_sb[:, cols(c)], func=ACT.Exp, bias=neg_chunk_max[:],
+                out=p_sb[:, cols(c)], in_=a_sb[:, cols(c)], func=ACT.Exp, bias=neg_chunk_max[:, c : c + 1],
                 accum_out=z_part[:, c : c + 1],
             )
         neg_max = column("neg_max")
-        nc.vector.tensor_reduce(out=neg_max[:], in_=chunk_max[:], axis=AX.X, op=ALU.max, negate=True)
+        nc.vector.tensor_reduce(out=neg_max[:], in_=neg_chunk_max[:], axis=AX.X, op=ALU.min)
 
         x_sb = keep.tile([P, I], F32, name="x_sb")
         nc.vector.tensor_tensor(x_sb[:], a_sb[:].indirect(offsets[:]), lpo_sb[:], ALU.subtract)
 
         lift = column("lift", CHUNKS)
-        nc.scalar.activation(out=lift[:], in_=chunk_max[:], func=ACT.Exp, bias=neg_max[:])
+        nc.scalar.activation(out=lift[:], in_=neg_chunk_max[:], func=ACT.Exp, scale=-1.0, bias=neg_max[:])
         z_lifted = column("z_lifted", CHUNKS)
         z = column("z")
         nc.vector.scalar_tensor_tensor(
             out=z_lifted[:], in0=z_part[:], scalar=1.0, in1=lift[:], op0=ALU.mult, op1=ALU.mult, accum_out=z[:]
         )
 
-        ta_sb = keep.tile([P, V], F32, name="ta_sb", tag="bias3")
+        ta_sb = keep.tile([P, V], F32, name="ta_sb", tag="max3", align_bytes=64)
         xp_sb = keep.tile([P, V], F32, name="xp_sb")
         xz_part = column("xz_part", CHUNKS)
         w_sb = keep.tile([P, I], F32, name="w_sb")
@@ -157,9 +158,9 @@ def tile_attend_hvpolicyratio_heads_kernel(tc, hid, voc_words, voc_scales, lpo, 
         rz = column("rz")
         nc.vector.reciprocal(out=rz[:], in_=z[:])
         neg_share = column("neg_share", CHUNKS)
-        nc.gpsimd.tensor_scalar(
-            out=neg_share[:], in0=lift[:], scalar1=rz[:], scalar2=-1.0, op0=ALU.mult, op1=ALU.mult
-        )
+        neg_rz = column("neg_rz")
+        nc.scalar.activation(out=neg_rz[:], in_=rz[:], func=ACT.Copy, scale=-1.0)
+        nc.scalar.activation(out=neg_share[:], in_=lift[:], func=ACT.Copy, scale=neg_rz[:])
         weigh_ta(1)
         copy_ta(0)
         copy_ta(1)
@@ -201,7 +202,7 @@ def tile_attend_hvpolicyratio_heads_kernel(tc, hid, voc_words, voc_scales, lpo, 
         t1 = keep.tile([P, V], F32, name="t1")
         for c in range(CHUNKS):
             nc.scalar.activation(out=t1[:, cols(c)], in_=xp_sb[:, cols(c)], func=ACT.Copy, scale=dz[:, c : c + 1])
-            turn_in(c, t1[:, cols(c)], False, False)
+            turn_in(c, t1[:, cols(c)], False, c < DIRECT)
 
         k = column("k")
         nc.scalar.activation(out=k[:], in_=s1[:], func=ACT.Identity, scale=neg_m[:], bias=s2[:])
@@ -212,15 +213,7 @@ def tile_attend_hvpolicyratio_heads_kernel(tc, hid, voc_words, voc_scales, lpo, 
         flat = keep.tile([P, V], F32, name="flat")
 
         def scale_p(c):
-            if c < 2:
-                nc.scalar.activation(
-                    out=t2[:, cols(c)], in_=p_sb[:, cols(c)], func=ACT.Copy, scale=xdz[:, c : c + 1]
-                )
-            else:
-                nc.gpsimd.tensor_scalar(
-                    out=t2[:, cols(c)], in0=p_sb[:, cols(c)], scalar1=k[:], scalar2=neg_share[:, c : c + 1],
-                    op0=ALU.mult, op1=ALU.mult,
-                )
+            nc.scalar.activation(out=t2[:, cols(c)], in_=p_sb[:, cols(c)], func=ACT.Copy, scale=xdz[:, c : c + 1])
             turn_in(c, t2[:, cols(c)], False, True)
 
         def finish(c):
@@ -230,11 +223,17 @@ def tile_attend_hvpolicyratio_heads_kernel(tc, hid, voc_words, voc_scales, lpo, 
                 lo = c * BANK + j * P
                 nc.tensor.transpose(back[:, j * P : (j + 1) * P], flat[:, lo : lo + P], ident[:])
             res = keep.tile([P, BANK], F32, name="res%d" % c)
-            nc.vector.tensor_tensor(res[:], back[:], xs1[:, cols(c)], ALU.add)
+            if c < DIRECT:
+                nc.vector.scalar_tensor_tensor(
+                    out=t2[:, cols(c)], in0=p_sb[:, cols(c)], scalar=xdz[:, c : c + 1], in1=back[:],
+                    op0=ALU.mult, op1=ALU.add,
+                )
+                nc.vector.tensor_tensor(res[:], t2[:, cols(c)], xs1[:, cols(c)], ALU.add)
+            else:
+                nc.vector.tensor_tensor(res[:], back[:], xs1[:, cols(c)], ALU.add)
             nc.sync.dma_start(out=out[:, cols(c)], in_=res[:])
 
-        scale_p(0)
         for c in range(CHUNKS):
-            if c + 1 < CHUNKS:
+            if DIRECT <= c + 1 < CHUNKS:
                 scale_p(c + 1)
             finish(c)

@@ -23,7 +23,6 @@ PACK = 4
 BANK = 512
 CHUNKS = V // BANK
 SPLIT = 112
-DIRECT = 1
 
 
 def tile_attend_hvpolicyratio_heads_kernel(tc, hid, voc_words, voc_scales, lpo, adv, dhid, base, offs, out):
@@ -77,7 +76,7 @@ def tile_attend_hvpolicyratio_heads_kernel(tc, hid, voc_words, voc_scales, lpo, 
             out=hid_bf[:, SPLIT:, :], in_=hid_raw[:, :, SPLIT:].rearrange("p j q -> p q j"), func=ACT.Copy
         )
         hid_q = quantise(hid_bf, "hid")
-        dhid_bf = keep.tile([P, Q, PACK], BF16, name="dhid_bf", tag="max1", align_bytes=64)
+        dhid_bf = keep.tile([P, Q, PACK], BF16, name="dhid_bf", tag="reused", align_bytes=64)
         nc.scalar.activation(out=dhid_bf[:], in_=dhid_raw[:].rearrange("p j q -> p q j"), func=ACT.Copy)
         dhid_q = quantise(dhid_bf, "dhid")
 
@@ -107,14 +106,16 @@ def tile_attend_hvpolicyratio_heads_kernel(tc, hid, voc_words, voc_scales, lpo, 
         p_sb = keep.tile([P, V], F32, name="p_sb")
         neg_chunk_max = column("neg_chunk_max", CHUNKS)
         z_part = column("z_part", CHUNKS)
+        max_first = column("max_first", CHUNKS - 1)
+        max_last = keep.tile([P, 1], F32, name="max_last", tag="reused", align_bytes=64)
         for c in range(CHUNKS):
-            chunk_max = keep.tile([P, 1], F32, name="chunk_max%d" % c, tag="max%d" % c, align_bytes=64)
+            chunk_max = max_first[:, c : c + 1] if c < CHUNKS - 1 else max_last[:]
             nc.vector.tensor_scalar(
                 out=a_sb[:, cols(c)], in0=a_ps[c][:], scalar1=1.0, scalar2=None,
-                op0=ALU.mult, op1=ALU.max, accum_out=chunk_max[:],
+                op0=ALU.mult, op1=ALU.max, accum_out=chunk_max,
             )
             nc.gpsimd.tensor_scalar(
-                out=neg_chunk_max[:, c : c + 1], in0=chunk_max[:], scalar1=-1.0, scalar2=0.0,
+                out=neg_chunk_max[:, c : c + 1], in0=chunk_max, scalar1=-1.0, scalar2=0.0,
                 op0=ALU.mult, op1=ALU.add,
             )
             nc.scalar.activation(
@@ -129,14 +130,13 @@ def tile_attend_hvpolicyratio_heads_kernel(tc, hid, voc_words, voc_scales, lpo, 
 
         lift = column("lift", CHUNKS)
         nc.scalar.activation(out=lift[:], in_=neg_chunk_max[:], func=ACT.Exp, scale=-1.0, bias=neg_max[:])
-        z_lifted = column("z_lifted", CHUNKS)
+        xp_sb = keep.tile([P, V], F32, name="xp_sb")
         z = column("z")
         nc.vector.scalar_tensor_tensor(
-            out=z_lifted[:], in0=z_part[:], scalar=1.0, in1=lift[:], op0=ALU.mult, op1=ALU.mult, accum_out=z[:]
+            out=xp_sb[:, BANK : BANK + CHUNKS], in0=z_part[:], scalar=1.0, in1=lift[:], op0=ALU.mult, op1=ALU.mult, accum_out=z[:]
         )
 
-        ta_sb = keep.tile([P, V], F32, name="ta_sb", tag="max3", align_bytes=64)
-        xp_sb = keep.tile([P, V], F32, name="xp_sb")
+        ta_sb = keep.tile([P, V], F32, name="ta_sb", tag="reused", align_bytes=64)
         xz_part = column("xz_part", CHUNKS)
         w_sb = keep.tile([P, I], F32, name="w_sb")
         s1 = column("s1")
@@ -176,7 +176,7 @@ def tile_attend_hvpolicyratio_heads_kernel(tc, hid, voc_words, voc_scales, lpo, 
             out=m_part[:], in0=xz_part[:], scalar=1.0, in1=neg_share[:], op0=ALU.mult, op1=ALU.mult,
             accum_out=neg_m[:],
         )
-        g_sb = keep.tile([P, I], F32, name="g_sb")
+        g_sb = keep.tile([P, I], F32, name="g_sb", tag="g_then_sum")
         nc.vector.tensor_tensor(g_sb[:], ta_sb[:].indirect(offsets[:]), w_sb[:], ALU.mult)
         xe1 = keep.tile([P, I], F32, name="xe1")
         s2 = column("s2")
@@ -185,7 +185,7 @@ def tile_attend_hvpolicyratio_heads_kernel(tc, hid, voc_words, voc_scales, lpo, 
         )
         nc.vector.tensor_copy(xs1[:].indirect(offsets[:]), xe1[:])
 
-        turned = [psum.tile([P, BANK], F32, name="turned%d" % c, tag="a_ps%d" % c) for c in range(CHUNKS)]
+        turned = {c: psum.tile([P, BANK], F32, name="turned%d" % c, tag="a_ps%d" % c) for c in range(1, CHUNKS)}
 
         def turn_in(c, src, start, stop):
             for j in range(BANK // P):
@@ -194,46 +194,58 @@ def tile_attend_hvpolicyratio_heads_kernel(tc, hid, voc_words, voc_scales, lpo, 
                     is_transpose=True, start=(start and j == 0), stop=(stop and j == BANK // P - 1),
                 )
 
-        for c in range(CHUNKS):
+        for c in range(1, CHUNKS):
             turn_in(c, base_sb[:, cols(c)], True, False)
 
         dz = column("dz", CHUNKS)
         nc.scalar.activation(out=dz[:], in_=neg_share[:], func=ACT.Copy, scale=s1[:])
         t1 = keep.tile([P, V], F32, name="t1")
-        for c in range(CHUNKS):
+        for c in (1, 2, 3, 0):
             nc.scalar.activation(out=t1[:, cols(c)], in_=xp_sb[:, cols(c)], func=ACT.Copy, scale=dz[:, c : c + 1])
-            turn_in(c, t1[:, cols(c)], False, c < DIRECT)
-
-        k = column("k")
-        nc.scalar.activation(out=k[:], in_=s1[:], func=ACT.Identity, scale=neg_m[:], bias=s2[:])
-
+            if c > 0:
+                turn_in(c, t1[:, cols(c)], False, False)
+        xdz_part = column("xdz_part", CHUNKS)
+        nc.scalar.activation(out=xdz_part[:], in_=dz[:], func=ACT.Copy, scale=neg_m[:])
         xdz = column("xdz", CHUNKS)
-        nc.scalar.activation(out=xdz[:], in_=neg_share[:], func=ACT.Copy, scale=k[:])
+        for c in (1, 2, 3, 0):
+            nc.scalar.activation(
+                out=xdz[:, c : c + 1], in_=neg_share[:, c : c + 1], func=ACT.Identity, scale=s2[:],
+                bias=xdz_part[:, c : c + 1],
+            )
         t2 = keep.tile([P, V], F32, name="t2")
         flat = keep.tile([P, V], F32, name="flat")
+        dense = {}
 
         def scale_p(c):
             nc.scalar.activation(out=t2[:, cols(c)], in_=p_sb[:, cols(c)], func=ACT.Copy, scale=xdz[:, c : c + 1])
             turn_in(c, t2[:, cols(c)], False, True)
 
-        def finish(c):
+        def add_on_gpsimd():
+            partial = keep.tile([P, BANK], F32, name="partial", tag="g_then_sum")
+            nc.gpsimd.tensor_tensor(partial[:], base_sb[:, cols(0)], t1[:, cols(0)], ALU.add)
+            nc.gpsimd.tensor_scalar(
+                out=t2[:, cols(0)], in0=p_sb[:, cols(0)], scalar1=xdz[:, 0:1], scalar2=0.0, op0=ALU.mult, op1=ALU.add
+            )
+            nc.gpsimd.tensor_tensor(flat[:, cols(0)], partial[:], t2[:, cols(0)], ALU.add)
+            dense[0] = flat[:, cols(0)]
+
+        def turn_back(c):
             nc.scalar.copy(out=flat[:, cols(c)], in_=turned[c][:])
             back = psum.tile([P, BANK], F32, name="back%d" % c, tag="ta_ps%d" % c)
             for j in range(BANK // P):
                 lo = c * BANK + j * P
                 nc.tensor.transpose(back[:, j * P : (j + 1) * P], flat[:, lo : lo + P], ident[:])
+            dense[c] = back[:]
+
+        def finish(c):
             res = keep.tile([P, BANK], F32, name="res%d" % c)
-            if c < DIRECT:
-                nc.vector.scalar_tensor_tensor(
-                    out=t2[:, cols(c)], in0=p_sb[:, cols(c)], scalar=xdz[:, c : c + 1], in1=back[:],
-                    op0=ALU.mult, op1=ALU.add,
-                )
-                nc.vector.tensor_tensor(res[:], t2[:, cols(c)], xs1[:, cols(c)], ALU.add)
-            else:
-                nc.vector.tensor_tensor(res[:], back[:], xs1[:, cols(c)], ALU.add)
+            nc.vector.tensor_tensor(res[:], dense[c], xs1[:, cols(c)], ALU.add)
             nc.sync.dma_start(out=out[:, cols(c)], in_=res[:])
 
-        for c in range(CHUNKS):
-            if DIRECT <= c + 1 < CHUNKS:
-                scale_p(c + 1)
+        add_on_gpsimd()
+        for c in range(1, CHUNKS):
+            scale_p(c)
+        for c in range(1, CHUNKS):
+            turn_back(c)
+        for c in (1, 0, 2, 3):
             finish(c)

from contextlib import ExitStack

import concourse.mybir as mybir
from concourse.masks import make_identity

D, V, Q, I = 512, 2048, 128, 512
FLOPS = 2 * 2 * D * Q * V

F32 = mybir.dt.float32
BF16 = mybir.dt.bfloat16
I32 = mybir.dt.int32
U32 = mybir.dt.uint32
U16 = mybir.dt.uint16
U8 = mybir.dt.uint8
FP8X4 = mybir.dt.float8_e4m3fn_x4
FP4X4 = mybir.dt.float4_e2m1fn_x4
ALU = mybir.AluOpType
ACT = mybir.ActivationFunctionType
AX = mybir.AxisListType

P = 128
PACK = 4
BANK = 512
CHUNKS = V // BANK
SPLIT = 112


def tile_attend_hvpolicyratio_heads_kernel(tc, hid, voc_words, voc_scales, lpo, adv, dhid, base, offs, out):
    nc = tc.nc
    with ExitStack() as ctx:
        keep = ctx.enter_context(tc.tile_pool(name="keep", bufs=1))
        psum = ctx.enter_context(tc.psum_pool(name="psum", bufs=1))

        voc_sc = keep.tile([P, V], U8, name="voc_sc", align_bytes=64)
        nc.vector.memset(voc_sc[:].bitcast(I32), 0)
        xs1 = keep.tile([P, V], F32, name="xs1")
        nc.vector.memset(xs1[:], 0.0)
        ident = keep.tile([P, P], F32, name="ident")
        make_identity(nc, ident[:])

        hid_raw = keep.tile([P, PACK, Q], F32, name="hid_raw")
        nc.sync.dma_start(out=hid_raw[:], in_=hid.rearrange("(p j) q -> p j q", j=PACK))
        halves = [keep.tile([P, V], U8, name="words%d" % h, align_bytes=64) for h in range(2)]
        nc.sync.dma_start(out=halves[0][:], in_=voc_words[0, :, 0:V])
        for quad in range(4):
            nc.sync.dma_start(
                out=voc_sc[32 * quad : 32 * quad + 4, :].bitcast(I32),
                in_=voc_scales[0, 4 * quad : 4 * quad + 4, :].bitcast(I32),
            )
        dhid_raw = keep.tile([P, PACK, Q], F32, name="dhid_raw")
        nc.sync.dma_start(out=dhid_raw[:], in_=dhid.rearrange("(p j) q -> p j q", j=PACK))
        nc.sync.dma_start(out=halves[1][:], in_=voc_words[0, :, V : 2 * V])
        words = [halves[c // 2][:, 2 * BANK * (c % 2) : 2 * BANK * (c % 2 + 1)] for c in range(CHUNKS)]
        offsets = keep.tile([P, I // 16], U16, name="offsets")
        nc.sync.dma_start(offsets[:], offs)

        lpo_sb = keep.tile([P, I], F32, name="lpo_sb")
        nc.sync.dma_start(out=lpo_sb[:], in_=lpo)
        adv_sb = keep.tile([P, I], F32, name="adv_sb")
        nc.sync.dma_start(out=adv_sb[:], in_=adv)
        base_sb = keep.tile([P, V], F32, name="base_sb")
        nc.sync.dma_start(out=base_sb[:], in_=base)


        def quantise(grouped, name):
            codes = keep.tile([P, Q], U32, name=name + "_codes", align_bytes=64)
            scales = keep.tile([P, Q], U8, name=name + "_scales", align_bytes=64)
            nc.vector.quantize_mx(
                out=codes[:].bitcast(FP8X4), scales=scales[:], in_=grouped[:].rearrange("p q j -> p (q j)")
            )
            return codes, scales

        hid_bf = keep.tile([P, Q, PACK], BF16, name="hid_bf", align_bytes=64)
        nc.vector.tensor_copy(out=hid_bf[:, :SPLIT, :], in_=hid_raw[:, :, :SPLIT].rearrange("p j q -> p q j"))
        nc.scalar.activation(
            out=hid_bf[:, SPLIT:, :], in_=hid_raw[:, :, SPLIT:].rearrange("p j q -> p q j"), func=ACT.Copy
        )
        hid_q = quantise(hid_bf, "hid")
        dhid_bf = keep.tile([P, Q, PACK], BF16, name="dhid_bf", tag="reused", align_bytes=64)
        nc.scalar.activation(out=dhid_bf[:], in_=dhid_raw[:].rearrange("p j q -> p q j"), func=ACT.Copy)
        dhid_q = quantise(dhid_bf, "dhid")

        def cols(c):
            return slice(c * BANK, (c + 1) * BANK)

        def score(q_operand, c, name):
            bank = psum.tile([P, BANK], F32, name=name, tag=name)
            nc.tensor.matmul_mx(
                out=bank[:],
                lhsT=q_operand[0][:].bitcast(FP8X4),
                lhsT_scale=q_operand[1][:],
                rhs=words[c].bitcast(FP4X4),
                rhs_scale=voc_sc[:, cols(c)],
                start=True,
                stop=True,
            )
            return bank

        a_ps = [score(hid_q, c, "a_ps%d" % c) for c in range(CHUNKS)]
        ta_ps = {c: score(dhid_q, c, "ta_ps%d" % c) for c in (2, 0, 3, 1)}

        def column(name, width=1):
            return keep.tile([P, width], F32, name=name)

        a_sb = keep.tile([P, V], F32, name="a_sb")
        p_sb = keep.tile([P, V], F32, name="p_sb")
        neg_chunk_max = column("neg_chunk_max", CHUNKS)
        z_part = column("z_part", CHUNKS)
        max_first = column("max_first", CHUNKS - 1)
        max_last = keep.tile([P, 1], F32, name="max_last", tag="reused", align_bytes=64)
        for c in range(CHUNKS):
            chunk_max = max_first[:, c : c + 1] if c < CHUNKS - 1 else max_last[:]
            nc.vector.tensor_scalar(
                out=a_sb[:, cols(c)], in0=a_ps[c][:], scalar1=1.0, scalar2=None,
                op0=ALU.mult, op1=ALU.max, accum_out=chunk_max,
            )
            nc.gpsimd.tensor_scalar(
                out=neg_chunk_max[:, c : c + 1], in0=chunk_max, scalar1=-1.0, scalar2=0.0,
                op0=ALU.mult, op1=ALU.add,
            )
            nc.scalar.activation(
                out=p_sb[:, cols(c)], in_=a_sb[:, cols(c)], func=ACT.Exp, bias=neg_chunk_max[:, c : c + 1],
                accum_out=z_part[:, c : c + 1],
            )
        neg_max = column("neg_max")
        nc.vector.tensor_reduce(out=neg_max[:], in_=neg_chunk_max[:], axis=AX.X, op=ALU.min)

        x_sb = keep.tile([P, I], F32, name="x_sb")
        nc.vector.tensor_tensor(x_sb[:], a_sb[:].indirect(offsets[:]), lpo_sb[:], ALU.subtract)

        lift = column("lift", CHUNKS)
        nc.scalar.activation(out=lift[:], in_=neg_chunk_max[:], func=ACT.Exp, scale=-1.0, bias=neg_max[:])
        xp_sb = keep.tile([P, V], F32, name="xp_sb")
        z = column("z")
        nc.vector.scalar_tensor_tensor(
            out=xp_sb[:, BANK : BANK + CHUNKS], in0=z_part[:], scalar=1.0, in1=lift[:], op0=ALU.mult, op1=ALU.mult, accum_out=z[:]
        )

        ta_sb = keep.tile([P, V], F32, name="ta_sb", tag="reused", align_bytes=64)
        xz_part = column("xz_part", CHUNKS)
        w_sb = keep.tile([P, I], F32, name="w_sb")
        s1 = column("s1")

        def copy_ta(c):
            nc.scalar.copy(out=ta_sb[:, cols(c)], in_=ta_ps[c][:])

        def weigh_ta(c):
            nc.vector.scalar_tensor_tensor(
                out=xp_sb[:, cols(c)], in0=ta_ps[c][:], scalar=1.0, in1=p_sb[:, cols(c)],
                op0=ALU.mult, op1=ALU.mult, accum_out=xz_part[:, c : c + 1],
            )

        r_sb = keep.tile([P, I], F32, name="r_sb")
        nc.scalar.activation(out=r_sb[:], in_=x_sb[:], func=ACT.Exp, bias=neg_max[:])
        copy_ta(2)
        copy_ta(3)
        weigh_ta(0)
        rz = column("rz")
        nc.vector.reciprocal(out=rz[:], in_=z[:])
        neg_share = column("neg_share", CHUNKS)
        neg_rz = column("neg_rz")
        nc.scalar.activation(out=neg_rz[:], in_=rz[:], func=ACT.Copy, scale=-1.0)
        nc.scalar.activation(out=neg_share[:], in_=lift[:], func=ACT.Copy, scale=neg_rz[:])
        weigh_ta(1)
        copy_ta(0)
        copy_ta(1)
        nc.vector.scalar_tensor_tensor(
            out=w_sb[:], in0=r_sb[:], scalar=rz[:], in1=adv_sb[:], op0=ALU.mult, op1=ALU.mult, accum_out=s1[:]
        )
        weigh_ta(2)
        weigh_ta(3)

        m_part = column("m_part", CHUNKS)
        neg_m = column("neg_m")
        nc.vector.scalar_tensor_tensor(
            out=m_part[:], in0=xz_part[:], scalar=1.0, in1=neg_share[:], op0=ALU.mult, op1=ALU.mult,
            accum_out=neg_m[:],
        )
        g_sb = keep.tile([P, I], F32, name="g_sb", tag="g_then_sum")
        nc.vector.tensor_tensor(g_sb[:], ta_sb[:].indirect(offsets[:]), w_sb[:], ALU.mult)
        xe1 = keep.tile([P, I], F32, name="xe1")
        s2 = column("s2")
        nc.vector.scalar_tensor_tensor(
            out=xe1[:], in0=w_sb[:], scalar=neg_m[:], in1=g_sb[:], op0=ALU.mult, op1=ALU.add, accum_out=s2[:]
        )
        nc.vector.tensor_copy(xs1[:].indirect(offsets[:]), xe1[:])

        turned = {c: psum.tile([P, BANK], F32, name="turned%d" % c, tag="a_ps%d" % c) for c in range(1, CHUNKS)}

        def turn_in(c, src, start, stop):
            for j in range(BANK // P):
                nc.tensor.matmul(
                    turned[c][:, j * P : (j + 1) * P], lhsT=src[:, j * P : (j + 1) * P], rhs=ident[:],
                    is_transpose=True, start=(start and j == 0), stop=(stop and j == BANK // P - 1),
                )

        for c in range(1, CHUNKS):
            turn_in(c, base_sb[:, cols(c)], True, False)

        dz = column("dz", CHUNKS)
        nc.scalar.activation(out=dz[:], in_=neg_share[:], func=ACT.Copy, scale=s1[:])
        t1 = keep.tile([P, V], F32, name="t1")
        for c in (1, 2, 3, 0):
            nc.scalar.activation(out=t1[:, cols(c)], in_=xp_sb[:, cols(c)], func=ACT.Copy, scale=dz[:, c : c + 1])
            if c > 0:
                turn_in(c, t1[:, cols(c)], False, False)
        xdz_part = column("xdz_part", CHUNKS)
        nc.scalar.activation(out=xdz_part[:], in_=dz[:], func=ACT.Copy, scale=neg_m[:])
        xdz = column("xdz", CHUNKS)
        for c in (1, 2, 3, 0):
            nc.scalar.activation(
                out=xdz[:, c : c + 1], in_=neg_share[:, c : c + 1], func=ACT.Identity, scale=s2[:],
                bias=xdz_part[:, c : c + 1],
            )
        t2 = keep.tile([P, V], F32, name="t2")
        flat = keep.tile([P, V], F32, name="flat")
        dense = {}

        def scale_p(c):
            nc.scalar.activation(out=t2[:, cols(c)], in_=p_sb[:, cols(c)], func=ACT.Copy, scale=xdz[:, c : c + 1])
            turn_in(c, t2[:, cols(c)], False, True)

        def add_on_gpsimd():
            partial = keep.tile([P, BANK], F32, name="partial", tag="g_then_sum")
            nc.gpsimd.tensor_tensor(partial[:], base_sb[:, cols(0)], t1[:, cols(0)], ALU.add)
            nc.gpsimd.tensor_scalar(
                out=t2[:, cols(0)], in0=p_sb[:, cols(0)], scalar1=xdz[:, 0:1], scalar2=0.0, op0=ALU.mult, op1=ALU.add
            )
            nc.gpsimd.tensor_tensor(flat[:, cols(0)], partial[:], t2[:, cols(0)], ALU.add)
            dense[0] = flat[:, cols(0)]

        def turn_back(c):
            nc.scalar.copy(out=flat[:, cols(c)], in_=turned[c][:])
            back = psum.tile([P, BANK], F32, name="back%d" % c, tag="ta_ps%d" % c)
            for j in range(BANK // P):
                lo = c * BANK + j * P
                nc.tensor.transpose(back[:, j * P : (j + 1) * P], flat[:, lo : lo + P], ident[:])
            dense[c] = back[:]

        def finish(c):
            res = keep.tile([P, BANK], F32, name="res%d" % c)
            nc.vector.tensor_tensor(res[:], dense[c], xs1[:, cols(c)], ALU.add)
            nc.sync.dma_start(out=out[:, cols(c)], in_=res[:])

        add_on_gpsimd()
        for c in range(1, CHUNKS):
            scale_p(c)
        for c in range(1, CHUNKS):
            turn_back(c)
        for c in (1, 0, 2, 3):
            finish(c)
